import numpy as np
import ml_dtypes


def mxq(x, axis, fmt="e4m3"):
    dtype, down = {"e4m3": (ml_dtypes.float8_e4m3fn, 7), "e5m2": (ml_dtypes.float8_e5m2, 14)}[fmt]
    v = np.moveaxis(np.asarray(x, np.float32).astype(ml_dtypes.bfloat16).astype(np.float64), axis, -1)
    blocks = v.reshape(v.shape[:-1] + (-1, 32))
    amax = np.abs(blocks).max(-1, keepdims=True)
    byte = np.maximum(np.where(amax > 0, np.frexp(amax)[1] - 1 + 127, 0) - down, 1)
    scale = np.exp2(byte - 127.0)
    codes = (blocks / scale).astype(np.float32).astype(dtype).astype(np.float64)
    return np.moveaxis((codes * scale).reshape(v.shape), -1, axis)


WIDE = False


def mx_kscale(k):
    if not WIDE:
        return np.ones(k)
    levels = np.array([10, -10, 5, -5, 0])
    if k % 512:
        return np.exp2(np.random.permutation(np.resize(levels, k // 32))).repeat(32)
    a = np.empty((k // 512, 16))
    for p in range(k // 512):
        a[p, :8] = np.random.permutation(np.resize(levels, 8))
        for g in range(8):
            far = levels[np.abs(levels - a[p, g]) >= 10]
            a[p, g + 8] = far[np.random.randint(len(far))]
    return np.exp2(a.ravel()).repeat(32)


def f64(x):
    return np.asarray(x).astype(np.float64)


def striped(idx):
    return np.tile(np.asarray(idx).reshape(-1, 16).T, (8, 1)).astype(np.uint16)


def unstriped(offs):
    return offs[:16].T.reshape(-1).astype(np.int64)


E2M1 = np.array([0.0, 0.5, 1.0, 1.5, 2.0, 3.0, 4.0, 6.0, -0.0, -0.5, -1.0, -1.5, -2.0, -3.0, -4.0, -6.0])


def pack_weight(w, fmt):
    k, n = w.shape
    w = f64(np.asarray(w, np.float32).astype(ml_dtypes.bfloat16)).reshape(k // 32, 32, n)
    amax = np.abs(w).max(1)
    if fmt == "e4m3":
        byte = np.frexp(amax)[1] - 1 + 127 - 7
    else:
        mant, ex = np.frexp(amax / 6.0)
        byte = np.where(mant > 0.5, ex, ex - 1) + 127
    byte = np.clip(np.where(amax > 0, byte, 1), 1, 254)
    scaled = (w * np.exp2(127.0 - byte)[:, None, :]).reshape(k, n).astype(np.float32)
    by_word = np.ascontiguousarray(scaled.reshape(k // 512, 128, 4, n).transpose(0, 1, 3, 2))
    if fmt == "e4m3":
        words = by_word.astype(ml_dtypes.float8_e4m3fn).view(np.uint8)
    else:
        c = by_word.astype(ml_dtypes.float4_e2m1fn).view(np.uint8) & 0xF
        words = (c[..., 0::2] | (c[..., 1::2] << 4)).reshape(k // 512, 128, 2 * n)
    return np.ascontiguousarray(words), np.ascontiguousarray(byte.astype(np.uint8).reshape(k // 512, 16, n))


def unpack_weight(words, scales, fmt):
    g, _, n = scales.shape
    words = np.ascontiguousarray(words).reshape(g, 128, n, -1)
    if fmt == "e4m3":
        vals = words.view(ml_dtypes.float8_e4m3fn).astype(np.float64)
    else:
        nib = np.empty((g, 128, n, 4), np.uint8)
        nib[..., 0::2] = words & 0xF
        nib[..., 1::2] = words >> 4
        vals = E2M1[nib]
    vals = vals * np.repeat(np.exp2(scales.astype(np.float64) - 127.0), 8, axis=1)[..., None]
    return vals.transpose(0, 1, 3, 2).reshape(g * 512, n)


D, E, T, I, Q = 512, 512, 2048, 512, 128


def setup_inputs():
    n = np.random.standard_normal
    idx = np.random.permutation(T)[:I]
    fd = mx_kscale(D)
    fe = mx_kscale(E)
    keysp = pack_weight(n((D, T)) / fd[:, None], "e4m3")
    valsp = pack_weight(n((E, T)) / fe[:, None], "e4m3")
    return {
        "query": (n((D, Q)) * 0.6 / np.sqrt(D) * fd[:, None]).astype(np.float32),
        "keys_words": keysp[0],
        "keys_scales": keysp[1],
        "lprior": np.tile(np.random.uniform(-7.5, -5.0, T), (128, 1)).astype(np.float32),
        "strict": (np.random.uniform(0.2, 0.8, (Q, 1))).astype(np.float32),
        "gout": (n((E, Q)) * 1 / np.sqrt(E) * fe[:, None]).astype(np.float32),
        "vals_words": valsp[0],
        "vals_scales": valsp[1],
        "old": (0.5 * n((Q, T))).astype(np.float32),
        "offs": striped(idx),
    }


def reference(query, keys_words, keys_scales, lprior, strict, gout, vals_words, vals_scales, old, offs):
    idx = unstriped(offs)
    keysu = unpack_weight(keys_words, keys_scales, "e4m3")
    valsu = unpack_weight(vals_words, vals_scales, "e4m3")
    queryq = mxq(f64(query), 0, "e4m3")
    keysidxg = keysu[:, idx]
    a = queryq.T @ keysidxg
    b = a - np.max(a, axis=1, keepdims=True)
    p = np.exp(b)
    z = np.sum(p, axis=1, keepdims=True)
    goutq = mxq(f64(gout), 0, "e4m3")
    valsidxg = valsu[:, idx]
    c0 = goutq.T @ valsidxg
    dz = f64(strict) / z - np.sum(p * c0, axis=1, keepdims=True) / np.square(z) - f64(strict) * (-1.0) * np.sum(p * (b - f64(lprior)[:1][:, idx]), axis=1, keepdims=True) / np.square(z)
    dp = 1.0 / z * c0 + f64(strict) * (-1.0) / z * (b - f64(lprior)[:1][:, idx]) + dz
    db = f64(strict) * (-1.0) / z * p + dp * p
    gs = db * 512.0
    gf = np.zeros((Q, T))
    gf[:, idx] = gs
    y = f64(old) + gf
    return y

@@ -1,0 +1,166 @@
+from contextlib import ExitStack
+
+import concourse.mybir as mybir
+from concourse.masks import make_identity
+
+D, E, T, I, Q = 512, 512, 2048, 512, 128
+FLOPS = 2 * Q * I * (D + E)
+
+F32 = mybir.dt.float32
+BF16 = mybir.dt.bfloat16
+I32 = mybir.dt.int32
+U32 = mybir.dt.uint32
+U16 = mybir.dt.uint16
+U8 = mybir.dt.uint8
+FP8X4 = mybir.dt.float8_e4m3fn_x4
+ALU = mybir.AluOpType
+ACT = mybir.ActivationFunctionType
+
+P = 128
+PACK = 4
+BANK = 512
+CHUNK = 512
+
+
+def tile_attend_bpriorpull_s_kernel(tc, query, keys_words, keys_scales, lprior, strict, gout, vals_words,
+                                     vals_scales, old, offs, out):
+    nc = tc.nc
+    with ExitStack() as ctx:
+        sb = ctx.enter_context(tc.tile_pool(name="sb", bufs=1))
+        ps = ctx.enter_context(tc.psum_pool(name="ps", bufs=1))
+
+        offsets = sb.tile([P, I // 16], U16, name="offsets")
+        nc.sync.dma_start(offsets[:], offs)
+
+        def load_scales(name, scales):
+            pool_bytes = sb.tile([P, T], U8, name=name, align_bytes=64)
+            nc.vector.memset(pool_bytes[:].bitcast(I32), 0)
+            for quad in range(4):
+                nc.sync.dma_start(out=pool_bytes[32 * quad : 32 * quad + 4, :].bitcast(I32),
+                                  in_=scales[0, 4 * quad : 4 * quad + 4, :].bitcast(I32))
+            return pool_bytes
+
+        def load_words(name, words):
+            pool_words = sb.tile([P, T], I32, name=name, tag=name, align_bytes=64)
+            nc.sync.dma_start(out=pool_words[:], in_=words[0].rearrange("p n t -> p (n t)").bitcast(I32))
+            return pool_words
+
+        def load_rows(name, rows):
+            raw = sb.tile([P, PACK, Q], F32, name=name)
+            nc.sync.dma_start(out=raw[:], in_=rows.rearrange("(p j) w -> p j w", j=PACK))
+            return raw
+
+        def interleave(name, raw):
+            grouped = sb.tile([P, Q, PACK], BF16, name=name, align_bytes=64)
+            nc.scalar.copy(out=grouped[:], in_=raw[:].rearrange("p j w -> p w j"))
+            return grouped
+
+        def quantize(name, grouped):
+            codes = sb.tile([P, Q], U32, name=name + "_codes", align_bytes=64)
+            scales = sb.tile([P, Q], U8, name=name + "_scales", align_bytes=64)
+            nc.vector.quantize_mx(out=codes[:].bitcast(FP8X4), scales=scales[:],
+                                  in_=grouped[:].rearrange("p w j -> p (w j)"))
+            return codes, scales
+
+        def gather(name, window, dtype):
+            picked = sb.tile([P, I], dtype, name=name, align_bytes=64)
+            nc.vector.tensor_copy(picked[:], window.indirect(offsets[:]))
+            return picked
+
+        ident = sb.tile([P, P], F32, name="ident")
+        make_identity(nc, ident[:])
+        lp_cols = sb.tile([P, T // P], F32, name="lp_cols")
+        nc.sync.dma_start(out=lp_cols[:], in_=lprior[0].rearrange("(p c) -> p c", p=P))
+
+        q_raw = load_rows("q_raw", query)
+        key_bytes = load_scales("key_bytes", keys_scales)
+        warm = sb.tile([P, 1], F32, name="warm")
+        warm_out = sb.tile([P, 1], F32, name="warm_out")
+        nc.vector.memset(warm[:], 0.0)
+        nc.scalar.activation(out=warm_out[:], in_=warm[:], func=ACT.Exp)
+
+        key_words = load_words("key_words", keys_words)
+        val_bytes = load_scales("val_bytes", vals_scales)
+
+        val_words = load_words("val_words", vals_words)
+        g_raw = load_rows("g_raw", gout)
+        s_col = sb.tile([P, 1], F32, name="s_col")
+        nc.sync.dma_start(out=s_col[:], in_=strict)
+        old_sb = sb.tile([P, T], F32, name="old_sb")
+        nc.sync.dma_start(out=old_sb[:], in_=old)
+
+        placed = sb.tile([P, T], F32, name="placed")
+        nc.vector.memset(placed[:], 0.0)
+
+        q_grouped = interleave("q_grouped", q_raw)
+        key_scales_g = gather("key_scales_g", key_bytes[:], U8)
+        q_codes, q_scales = quantize("q", q_grouped)
+
+        lp_win = sb.tile([P, T], F32, name="lp_win")
+        lp_view = lp_win[:].rearrange("p (j b c) -> p b j c", b=4, c=4)
+        for b in range(4):
+            bank = ps.tile([P, 4, P], F32, name="lp_bank%d" % b)
+            for c in range(4):
+                col = 4 * b + c
+                nc.tensor.transpose(bank[:, c, :], lp_cols[:, col : col + 1].to_broadcast([P, P]), ident[:])
+            nc.scalar.activation(out=lp_view[:, b], in_=bank[:].rearrange("p c j -> p j c"), func=ACT.Copy)
+
+        key_words_g = gather("key_words_g", key_words[:].bitcast(U32), U32)
+        a_ps = ps.tile([P, I], F32, name="a_ps")
+        nc.tensor.matmul_mx(out=a_ps[:], lhsT=q_codes[:].bitcast(FP8X4), lhsT_scale=q_scales[:],
+                            rhs=key_words_g[:].bitcast(FP8X4), rhs_scale=key_scales_g[:], start=True, stop=True)
+
+        g_grouped = interleave("g_grouped", g_raw)
+        val_scales_g = gather("val_scales_g", val_bytes[:], U8)
+        g_codes, g_scales = quantize("g", g_grouped)
+
+        neg_a = sb.tile([P, I], F32, name="neg_a")
+        neg_max = sb.tile([P, 1], F32, name="neg_max")
+        nc.vector.tensor_scalar(out=neg_a[:], in0=a_ps[:], scalar1=-1.0, scalar2=None, op0=ALU.mult, op1=ALU.min,
+                                accum_out=neg_max[:])
+        p = sb.tile([P, I], F32, name="p")
+        z = sb.tile([P, 1], F32, name="z")
+        nc.scalar.activation(out=p[:], in_=neg_a[:], func=ACT.Exp, bias=neg_max[:], scale=-1.0, accum_out=z[:])
+
+        halves = [slice(0, I // 2), slice(I // 2, I)]
+        lists = [offsets[:, 0 : I // 32], offsets[:, I // 32 : I // 16]]
+        u0 = sb.tile([P, I // 2], F32, name="u0")
+        nc.vector.tensor_tensor(u0[:], lp_win[:].indirect(lists[0]), neg_a[:, halves[0]], ALU.add)
+
+        val_words_g = gather("val_words_g", val_words[:].bitcast(U32), U32)
+        c_ps = [ps.tile([P, I // 2], F32, name="c_ps%d" % k) for k in range(2)]
+        for k in range(2):
+            nc.tensor.matmul_mx(out=c_ps[k][:], lhsT=g_codes[:].bitcast(FP8X4), lhsT_scale=g_scales[:],
+                                rhs=val_words_g[:, halves[k]].bitcast(FP8X4), rhs_scale=val_scales_g[:, halves[k]],
+                                start=True, stop=True)
+
+        u1 = sb.tile([P, I // 2], F32, name="u1", tag="val_words", align_bytes=64)
+        nc.vector.tensor_tensor(u1[:], lp_win[:].indirect(lists[1]), neg_a[:, halves[1]], ALU.add)
+
+        rz = sb.tile([P, 1], F32, name="rz")
+        nc.vector.reciprocal(rz[:], z[:])
+        rz_i = sb.tile([P, 1], F32, name="rz_i")
+        nc.scalar.activation(out=rz_i[:], in_=rz[:], func=ACT.Copy, scale=float(I))
+        w = sb.tile([P, I], F32, name="w")
+        nc.scalar.activation(out=w[:], in_=p[:], func=ACT.Copy, scale=rz_i[:])
+
+        h = sb.tile([P, I], F32, name="h")
+        for k, u in enumerate((u0, u1)):
+            nc.vector.scalar_tensor_tensor(out=h[:, halves[k]], in0=u[:], scalar=s_col[:], in1=c_ps[k][:],
+                                           op0=ALU.mult, op1=ALU.add)
+        wh = sb.tile([P, I], F32, name="wh")
+        h_mean = sb.tile([P, 2], F32, name="h_mean")
+        for k in range(2):
+            nc.vector.scalar_tensor_tensor(out=wh[:, halves[k]], in0=h[:, halves[k]], scalar=1.0 / I,
+                                           in1=w[:, halves[k]], op0=ALU.mult, op1=ALU.mult,
+                                           accum_out=h_mean[:, k : k + 1])
+        centred = sb.tile([P, I], F32, name="centred")
+        nc.vector.tensor_scalar(out=centred[:], in0=h[:], scalar1=h_mean[:, 0:1], scalar2=h_mean[:, 1:2],
+                                op0=ALU.subtract, op1=ALU.subtract)
+        nc.vector.tensor_tensor(placed[:].indirect(offsets[:]), centred[:], w[:], ALU.mult)
+
+        for k in range(T // CHUNK):
+            cols = slice(k * CHUNK, (k + 1) * CHUNK)
+            res = sb.tile([P, CHUNK], F32, name="res%d" % k)
+            nc.vector.tensor_tensor(res[:], placed[:, cols], old_sb[:, cols], ALU.add)
+            nc.sync.dma_start(out=out[:, cols], in_=res[:])

@@ -19,7 +19,7 @@ ACT = mybir.ActivationFunctionType
 P = 128
 PACK = 4
 BANK = 512
-CHUNK = 512
+CHUNKS = (256, 512, 512, 512, 256)
 
 
 def tile_attend_bpriorpull_s_kernel(tc, query, keys_words, keys_scales, lprior, strict, gout, vals_words,
@@ -32,11 +32,11 @@ def tile_attend_bpriorpull_s_kernel(tc, query, keys_words, keys_scales, lprior, 
         offsets = sb.tile([P, I // 16], U16, name="offsets")
         nc.sync.dma_start(offsets[:], offs)
 
-        def load_scales(name, scales):
+        def load_scales(name, scales, first):
             pool_bytes = sb.tile([P, T], U8, name=name, align_bytes=64)
             nc.vector.memset(pool_bytes[:].bitcast(I32), 0)
             for quad in range(4):
-                nc.sync.dma_start(out=pool_bytes[32 * quad : 32 * quad + 4, :].bitcast(I32),
+                nc.sync.dma_start(out=pool_bytes[32 * quad + first : 32 * quad + first + 4, :].bitcast(I32),
                                   in_=scales[0, 4 * quad : 4 * quad + 4, :].bitcast(I32))
             return pool_bytes
 
@@ -73,24 +73,24 @@ def tile_attend_bpriorpull_s_kernel(tc, query, keys_words, keys_scales, lprior, 
         nc.sync.dma_start(out=lp_cols[:], in_=lprior[0].rearrange("(p c) -> p c", p=P))
 
         q_raw = load_rows("q_raw", query)
-        key_bytes = load_scales("key_bytes", keys_scales)
+        key_bytes = load_scales("key_bytes", keys_scales, 0)
         warm = sb.tile([P, 1], F32, name="warm")
         warm_out = sb.tile([P, 1], F32, name="warm_out")
         nc.vector.memset(warm[:], 0.0)
         nc.scalar.activation(out=warm_out[:], in_=warm[:], func=ACT.Exp)
 
         key_words = load_words("key_words", keys_words)
-        val_bytes = load_scales("val_bytes", vals_scales)
+        val_bytes = load_scales("val_bytes", vals_scales, 4)
 
-        val_words = load_words("val_words", vals_words)
         g_raw = load_rows("g_raw", gout)
+        val_words = load_words("val_words", vals_words)
         s_col = sb.tile([P, 1], F32, name="s_col")
         nc.sync.dma_start(out=s_col[:], in_=strict)
         old_sb = sb.tile([P, T], F32, name="old_sb")
         nc.sync.dma_start(out=old_sb[:], in_=old)
 
         placed = sb.tile([P, T], F32, name="placed")
-        nc.vector.memset(placed[:], 0.0)
+        nc.vector.memset(placed[:].bitcast(I32), 0)
 
         q_grouped = interleave("q_grouped", q_raw)
         key_scales_g = gather("key_scales_g", key_bytes[:], U8)
@@ -131,7 +131,7 @@ def tile_attend_bpriorpull_s_kernel(tc, query, keys_words, keys_scales, lprior, 
         c_ps = [ps.tile([P, I // 2], F32, name="c_ps%d" % k) for k in range(2)]
         for k in range(2):
             nc.tensor.matmul_mx(out=c_ps[k][:], lhsT=g_codes[:].bitcast(FP8X4), lhsT_scale=g_scales[:],
-                                rhs=val_words_g[:, halves[k]].bitcast(FP8X4), rhs_scale=val_scales_g[:, halves[k]],
+                                rhs=val_words_g[:, halves[k]].bitcast(FP8X4), rhs_scale=val_scales_g[4:P, halves[k]],
                                 start=True, stop=True)
 
         u1 = sb.tile([P, I // 2], F32, name="u1", tag="val_words", align_bytes=64)
@@ -159,8 +159,10 @@ def tile_attend_bpriorpull_s_kernel(tc, query, keys_words, keys_scales, lprior, 
                                 op0=ALU.subtract, op1=ALU.subtract)
         nc.vector.tensor_tensor(placed[:].indirect(offsets[:]), centred[:], w[:], ALU.mult)
 
-        for k in range(T // CHUNK):
-            cols = slice(k * CHUNK, (k + 1) * CHUNK)
-            res = sb.tile([P, CHUNK], F32, name="res%d" % k)
+        start = 0
+        for k, width in enumerate(CHUNKS):
+            cols = slice(start, start + width)
+            start = start + width
+            res = sb.tile([P, width], F32, name="res%d" % k)
             nc.vector.tensor_tensor(res[:], placed[:, cols], old_sb[:, cols], ALU.add)
-            nc.sync.dma_start(out=out[:, cols], in_=res[:])
+            (nc.sync, nc.scalar)[k % 2].dma_start(out=out[:, cols], in_=res[:])

from contextlib import ExitStack

import concourse.mybir as mybir
from concourse.masks import make_identity

D, E, T, I, Q = 512, 512, 2048, 512, 128
FLOPS = 2 * Q * I * (D + E)

F32 = mybir.dt.float32
BF16 = mybir.dt.bfloat16
I32 = mybir.dt.int32
U32 = mybir.dt.uint32
U16 = mybir.dt.uint16
U8 = mybir.dt.uint8
FP8X4 = mybir.dt.float8_e4m3fn_x4
ALU = mybir.AluOpType
ACT = mybir.ActivationFunctionType

P = 128
PACK = 4
BANK = 512
CHUNKS = (256, 512, 512, 512, 256)


def tile_attend_bpriorpull_s_kernel(tc, query, keys_words, keys_scales, lprior, strict, gout, vals_words,
                                     vals_scales, old, offs, out):
    nc = tc.nc
    with ExitStack() as ctx:
        sb = ctx.enter_context(tc.tile_pool(name="sb", bufs=1))
        ps = ctx.enter_context(tc.psum_pool(name="ps", bufs=1))

        offsets = sb.tile([P, I // 16], U16, name="offsets")
        nc.sync.dma_start(offsets[:], offs)

        def load_scales(name, scales, first):
            pool_bytes = sb.tile([P, T], U8, name=name, align_bytes=64)
            nc.vector.memset(pool_bytes[:].bitcast(I32), 0)
            for quad in range(4):
                nc.sync.dma_start(out=pool_bytes[32 * quad + first : 32 * quad + first + 4, :].bitcast(I32),
                                  in_=scales[0, 4 * quad : 4 * quad + 4, :].bitcast(I32))
            return pool_bytes

        def load_words(name, words):
            pool_words = sb.tile([P, T], I32, name=name, tag=name, align_bytes=64)
            nc.sync.dma_start(out=pool_words[:], in_=words[0].rearrange("p n t -> p (n t)").bitcast(I32))
            return pool_words

        def load_rows(name, rows):
            raw = sb.tile([P, PACK, Q], F32, name=name)
            nc.sync.dma_start(out=raw[:], in_=rows.rearrange("(p j) w -> p j w", j=PACK))
            return raw

        def interleave(name, raw):
            grouped = sb.tile([P, Q, PACK], BF16, name=name, align_bytes=64)
            nc.scalar.copy(out=grouped[:], in_=raw[:].rearrange("p j w -> p w j"))
            return grouped

        def quantize(name, grouped):
            codes = sb.tile([P, Q], U32, name=name + "_codes", align_bytes=64)
            scales = sb.tile([P, Q], U8, name=name + "_scales", align_bytes=64)
            nc.vector.quantize_mx(out=codes[:].bitcast(FP8X4), scales=scales[:],
                                  in_=grouped[:].rearrange("p w j -> p (w j)"))
            return codes, scales

        def gather(name, window, dtype):
            picked = sb.tile([P, I], dtype, name=name, align_bytes=64)
            nc.vector.tensor_copy(picked[:], window.indirect(offsets[:]))
            return picked

        ident = sb.tile([P, P], F32, name="ident")
        make_identity(nc, ident[:])
        lp_cols = sb.tile([P, T // P], F32, name="lp_cols")
        nc.sync.dma_start(out=lp_cols[:], in_=lprior[0].rearrange("(p c) -> p c", p=P))

        q_raw = load_rows("q_raw", query)
        key_bytes = load_scales("key_bytes", keys_scales, 0)
        warm = sb.tile([P, 1], F32, name="warm")
        warm_out = sb.tile([P, 1], F32, name="warm_out")
        nc.vector.memset(warm[:], 0.0)
        nc.scalar.activation(out=warm_out[:], in_=warm[:], func=ACT.Exp)

        key_words = load_words("key_words", keys_words)
        val_bytes = load_scales("val_bytes", vals_scales, 4)

        g_raw = load_rows("g_raw", gout)
        val_words = load_words("val_words", vals_words)
        s_col = sb.tile([P, 1], F32, name="s_col")
        nc.sync.dma_start(out=s_col[:], in_=strict)
        old_sb = sb.tile([P, T], F32, name="old_sb")
        nc.sync.dma_start(out=old_sb[:], in_=old)

        placed = sb.tile([P, T], F32, name="placed")
        nc.vector.memset(placed[:].bitcast(I32), 0)

        q_grouped = interleave("q_grouped", q_raw)
        key_scales_g = gather("key_scales_g", key_bytes[:], U8)
        q_codes, q_scales = quantize("q", q_grouped)

        lp_win = sb.tile([P, T], F32, name="lp_win")
        lp_view = lp_win[:].rearrange("p (j b c) -> p b j c", b=4, c=4)
        for b in range(4):
            bank = ps.tile([P, 4, P], F32, name="lp_bank%d" % b)
            for c in range(4):
                col = 4 * b + c
                nc.tensor.transpose(bank[:, c, :], lp_cols[:, col : col + 1].to_broadcast([P, P]), ident[:])
            nc.scalar.activation(out=lp_view[:, b], in_=bank[:].rearrange("p c j -> p j c"), func=ACT.Copy)

        key_words_g = gather("key_words_g", key_words[:].bitcast(U32), U32)
        a_ps = ps.tile([P, I], F32, name="a_ps")
        nc.tensor.matmul_mx(out=a_ps[:], lhsT=q_codes[:].bitcast(FP8X4), lhsT_scale=q_scales[:],
                            rhs=key_words_g[:].bitcast(FP8X4), rhs_scale=key_scales_g[:], start=True, stop=True)

        g_grouped = interleave("g_grouped", g_raw)
        val_scales_g = gather("val_scales_g", val_bytes[:], U8)
        g_codes, g_scales = quantize("g", g_grouped)

        neg_a = sb.tile([P, I], F32, name="neg_a")
        neg_max = sb.tile([P, 1], F32, name="neg_max")
        nc.vector.tensor_scalar(out=neg_a[:], in0=a_ps[:], scalar1=-1.0, scalar2=None, op0=ALU.mult, op1=ALU.min,
                                accum_out=neg_max[:])
        p = sb.tile([P, I], F32, name="p")
        z = sb.tile([P, 1], F32, name="z")
        nc.scalar.activation(out=p[:], in_=neg_a[:], func=ACT.Exp, bias=neg_max[:], scale=-1.0, accum_out=z[:])

        halves = [slice(0, I // 2), slice(I // 2, I)]
        lists = [offsets[:, 0 : I // 32], offsets[:, I // 32 : I // 16]]
        u0 = sb.tile([P, I // 2], F32, name="u0")
        nc.vector.tensor_tensor(u0[:], lp_win[:].indirect(lists[0]), neg_a[:, halves[0]], ALU.add)

        val_words_g = gather("val_words_g", val_words[:].bitcast(U32), U32)
        c_ps = [ps.tile([P, I // 2], F32, name="c_ps%d" % k) for k in range(2)]
        for k in range(2):
            nc.tensor.matmul_mx(out=c_ps[k][:], lhsT=g_codes[:].bitcast(FP8X4), lhsT_scale=g_scales[:],
                                rhs=val_words_g[:, halves[k]].bitcast(FP8X4), rhs_scale=val_scales_g[4:P, halves[k]],
                                start=True, stop=True)

        u1 = sb.tile([P, I // 2], F32, name="u1", tag="val_words", align_bytes=64)
        nc.vector.tensor_tensor(u1[:], lp_win[:].indirect(lists[1]), neg_a[:, halves[1]], ALU.add)

        rz = sb.tile([P, 1], F32, name="rz")
        nc.vector.reciprocal(rz[:], z[:])
        rz_i = sb.tile([P, 1], F32, name="rz_i")
        nc.scalar.activation(out=rz_i[:], in_=rz[:], func=ACT.Copy, scale=float(I))
        w = sb.tile([P, I], F32, name="w")
        nc.scalar.activation(out=w[:], in_=p[:], func=ACT.Copy, scale=rz_i[:])

        h = sb.tile([P, I], F32, name="h")
        for k, u in enumerate((u0, u1)):
            nc.vector.scalar_tensor_tensor(out=h[:, halves[k]], in0=u[:], scalar=s_col[:], in1=c_ps[k][:],
                                           op0=ALU.mult, op1=ALU.add)
        wh = sb.tile([P, I], F32, name="wh")
        h_mean = sb.tile([P, 2], F32, name="h_mean")
        for k in range(2):
            nc.vector.scalar_tensor_tensor(out=wh[:, halves[k]], in0=h[:, halves[k]], scalar=1.0 / I,
                                           in1=w[:, halves[k]], op0=ALU.mult, op1=ALU.mult,
                                           accum_out=h_mean[:, k : k + 1])
        centred = sb.tile([P, I], F32, name="centred")
        nc.vector.tensor_scalar(out=centred[:], in0=h[:], scalar1=h_mean[:, 0:1], scalar2=h_mean[:, 1:2],
                                op0=ALU.subtract, op1=ALU.subtract)
        nc.vector.tensor_tensor(placed[:].indirect(offsets[:]), centred[:], w[:], ALU.mult)

        start = 0
        for k, width in enumerate(CHUNKS):
            cols = slice(start, start + width)
            start = start + width
            res = sb.tile([P, width], F32, name="res%d" % k)
            nc.vector.tensor_tensor(res[:], placed[:, cols], old_sb[:, cols], ALU.add)
            (nc.sync, nc.scalar)[k % 2].dma_start(out=out[:, cols], in_=res[:])
